import numpy as np
import ml_dtypes


def mxq(x, axis, fmt="e4m3"):
    dtype, down = {"e4m3": (ml_dtypes.float8_e4m3fn, 7), "e5m2": (ml_dtypes.float8_e5m2, 14)}[fmt]
    v = np.moveaxis(np.asarray(x, np.float32).astype(ml_dtypes.bfloat16).astype(np.float64), axis, -1)
    blocks = v.reshape(v.shape[:-1] + (-1, 32))
    amax = np.abs(blocks).max(-1, keepdims=True)
    byte = np.maximum(np.where(amax > 0, np.frexp(amax)[1] - 1 + 127, 0) - down, 1)
    scale = np.exp2(byte - 127.0)
    codes = (blocks / scale).astype(np.float32).astype(dtype).astype(np.float64)
    return np.moveaxis((codes * scale).reshape(v.shape), -1, axis)


WIDE = False


def mx_kscale(k):
    if not WIDE:
        return np.ones(k)
    levels = np.array([10, -10, 5, -5, 0])
    if k % 512:
        return np.exp2(np.random.permutation(np.resize(levels, k // 32))).repeat(32)
    a = np.empty((k // 512, 16))
    for p in range(k // 512):
        a[p, :8] = np.random.permutation(np.resize(levels, 8))
        for g in range(8):
            far = levels[np.abs(levels - a[p, g]) >= 10]
            a[p, g + 8] = far[np.random.randint(len(far))]
    return np.exp2(a.ravel()).repeat(32)


def f64(x):
    return np.asarray(x).astype(np.float64)


E2M1 = np.array([0.0, 0.5, 1.0, 1.5, 2.0, 3.0, 4.0, 6.0, -0.0, -0.5, -1.0, -1.5, -2.0, -3.0, -4.0, -6.0])


def pack_weight(w, fmt):
    k, n = w.shape
    w = f64(np.asarray(w, np.float32).astype(ml_dtypes.bfloat16)).reshape(k // 32, 32, n)
    amax = np.abs(w).max(1)
    if fmt == "e4m3":
        byte = np.frexp(amax)[1] - 1 + 127 - 7
    else:
        mant, ex = np.frexp(amax / 6.0)
        byte = np.where(mant > 0.5, ex, ex - 1) + 127
    byte = np.clip(np.where(amax > 0, byte, 1), 1, 254)
    scaled = (w * np.exp2(127.0 - byte)[:, None, :]).reshape(k, n).astype(np.float32)
    by_word = np.ascontiguousarray(scaled.reshape(k // 512, 128, 4, n).transpose(0, 1, 3, 2))
    if fmt == "e4m3":
        words = by_word.astype(ml_dtypes.float8_e4m3fn).view(np.uint8)
    else:
        c = by_word.astype(ml_dtypes.float4_e2m1fn).view(np.uint8) & 0xF
        words = (c[..., 0::2] | (c[..., 1::2] << 4)).reshape(k // 512, 128, 2 * n)
    return np.ascontiguousarray(words), np.ascontiguousarray(byte.astype(np.uint8).reshape(k // 512, 16, n))


def unpack_weight(words, scales, fmt):
    g, _, n = scales.shape
    words = np.ascontiguousarray(words).reshape(g, 128, n, -1)
    if fmt == "e4m3":
        vals = words.view(ml_dtypes.float8_e4m3fn).astype(np.float64)
    else:
        nib = np.empty((g, 128, n, 4), np.uint8)
        nib[..., 0::2] = words & 0xF
        nib[..., 1::2] = words >> 4
        vals = E2M1[nib]
    vals = vals * np.repeat(np.exp2(scales.astype(np.float64) - 127.0), 8, axis=1)[..., None]
    return vals.transpose(0, 1, 3, 2).reshape(g * 512, n)


def silu(v):
    return v / (1.0 + np.exp(-np.maximum(v, -700.0)))


D, K, M, T = 256, 512, 512, 1024


def setup_inputs():
    n = np.random.standard_normal
    s = mx_kscale(K)[:, None]
    p_w0 = pack_weight(n((K, M)) / np.sqrt(K) / s, "e2m1")
    p_w1 = pack_weight(n((K, M)) / np.sqrt(K) / s, "e4m3")
    return {
        "x": (n((K, T + 2 * D)) * s).astype(np.float32),
        "w0_words": p_w0[0],
        "w0_scales": p_w0[1],
        "w1_words": p_w1[0],
        "w1_scales": p_w1[1],
        "w2": (n((K, M)) / np.sqrt(K) / s).astype(np.float32),
        "b": (0.3 * n(512)).astype(np.float32),
    }


def reference(x, w0_words, w0_scales, w1_words, w1_scales, w2, b):
    x_ = mxq(f64(x), 0, "e4m3")
    w0_ = unpack_weight(w0_words, w0_scales, "e2m1")
    w1_ = unpack_weight(w1_words, w1_scales, "e4m3")
    w2_ = mxq(f64(w2), 0, "e4m3")
    y = w0_.T @ x_[:, :T] + w1_.T @ x_[:, D:D + T] + w2_.T @ x_[:, 2 * D:]
    return silu(y + f64(b)[:, None])

@@ -1,0 +1,170 @@
+from contextlib import ExitStack
+
+import concourse.mybir as mybir
+from concourse.masks import make_identity
+
+D, K, M, T = 256, 512, 512, 1024
+FLOPS = 2 * 3 * K * M * T
+
+F32 = mybir.dt.float32
+BF16 = mybir.dt.bfloat16
+I32 = mybir.dt.int32
+U32 = mybir.dt.uint32
+U8 = mybir.dt.uint8
+FP8X4 = mybir.dt.float8_e4m3fn_x4
+FP4X4 = mybir.dt.float4_e2m1fn_x4
+SILU = mybir.ActivationFunctionType.Silu
+
+P = 128
+PACK = 4
+M_TILES = M // P
+X_COLS = T + 2 * D
+
+
+def tile_mix_dconv_fm_silu_kernel(tc, x, w0_words, w0_scales, w1_words, w1_scales, w2, b, out):
+    nc = tc.nc
+    x_rows = x.rearrange("(p j) t -> p j t", j=PACK)
+    w2_rows = w2.rearrange("(p j) n -> p j n", j=PACK)
+    out_tiles = out.rearrange("(m p) t -> p m t", p=P)
+
+    with ExitStack() as ctx:
+        sb = ctx.enter_context(tc.tile_pool(name="sb", bufs=1))
+        ps = ctx.enter_context(tc.psum_pool(name="ps", bufs=1))
+        ctx.enter_context(tc.manual_schedule())
+
+        x_codes = sb.tile([P, X_COLS], U32, align_bytes=64)
+        x_scale = sb.tile([P, X_COLS], U8, align_bytes=64)
+        w0_codes = sb.tile([P, 2 * M], U8, align_bytes=64)
+        w0_scale = sb.tile([P, M], U8, align_bytes=64)
+        w1_codes = sb.tile([P, M], U32, align_bytes=64)
+        w1_scale = sb.tile([P, M], U8, align_bytes=64)
+        w2_codes = sb.tile([P, M], U32, align_bytes=64)
+        w2_scale = sb.tile([P, M], U8, align_bytes=64)
+        bias_rows = sb.tile([P, P], F32)
+        bias = sb.tile([P, M_TILES], F32)
+        ident = sb.tile([P, P], F32)
+        warm = sb.tile([P, 1], F32)
+
+        def load(rows, c0, c1, name):
+            raw = sb.tile([P, PACK, c1 - c0], F32, name=name)
+            nc.sync.dma_start(out=raw[:], in_=rows[:, :, c0:c1])
+            return raw
+
+        def load_scales(queue, plane, scales):
+            for r in range(4):
+                queue.dma_start(out=plane[r:P:32, :].bitcast(I32), in_=scales[0, r:16:4, :].bitcast(I32))
+
+        def interleave(raw, c0, c1, name):
+            packed = sb.tile([P, PACK * (c1 - c0)], BF16, name=name, align_bytes=64)
+            nc.vector.tensor_copy(
+                out=packed[:].rearrange("p (c i j) -> p c j i", i=4, j=PACK),
+                in_=raw[:, :, c0:c1].rearrange("p j (c i) -> p c j i", i=4),
+            )
+            return packed
+
+        def quantise(packed, codes, scale, c0):
+            cols = slice(c0, c0 + packed.shape[1] // PACK)
+            nc.vector.quantize_mx(out=codes[:, cols].bitcast(FP8X4), scales=scale[:, cols], in_=packed[:])
+
+        def prepare(raw, codes, scale, c0, name):
+            half = raw.shape[2] // 2
+            packed = [interleave(raw, h * half, (h + 1) * half, "%s_%d" % (name, h)) for h in range(2)]
+            for h in range(2):
+                quantise(packed[h], codes, scale, c0 + h * half)
+
+        def tap(acc, t_base, which, m, t0, t1, start=False, stop=False):
+            m_cols = slice(m * P, (m + 1) * P)
+            if which == 0:
+                lhs, lhs_scale = w0_codes[:, 2 * m * P:2 * (m + 1) * P].bitcast(FP4X4), w0_scale[:, m_cols]
+            elif which == 1:
+                lhs, lhs_scale = w1_codes[:, m_cols].bitcast(FP8X4), w1_scale[:, m_cols]
+            else:
+                lhs, lhs_scale = w2_codes[:, m_cols].bitcast(FP8X4), w2_scale[:, m_cols]
+            x_cols = slice(t0 + which * D, t1 + which * D)
+            nc.tensor.matmul_mx(
+                out=acc[:, t0 - t_base:t1 - t_base], lhsT=lhs, lhsT_scale=lhs_scale,
+                rhs=x_codes[:, x_cols].bitcast(FP8X4), rhs_scale=x_scale[:, x_cols], start=start, stop=stop,
+            )
+
+        def finish(accs, m0, m1, t0, t1, name):
+            res = sb.tile([P, m1 - m0, t1 - t0], F32, name=name)
+            for m in range(m0, m1):
+                nc.scalar.activation(out=res[:, m - m0, :], in_=accs[m][:], func=SILU, bias=bias[:, m:m + 1])
+            nc.sync.dma_start(out=out_tiles[:, m0:m1, t0:t1], in_=res[:])
+
+        nc.vector.memset(bias_rows[:], 0.0)
+        nc.vector.memset(w0_scale[:].bitcast(I32), 0)
+        nc.vector.memset(w1_scale[:].bitcast(I32), 0)
+        nc.vector.memset(warm[:], 0.0)
+        nc.scalar.activation(out=warm[:], in_=warm[:], func=SILU)
+        make_identity(nc, ident[:])
+        nc.gpsimd.dma_start(out=bias_rows[0:M_TILES, :], in_=b.rearrange("(m p) -> m p", p=P))
+        load_scales(nc.gpsimd, w0_scale, w0_scales)
+
+        x01 = load(x_rows, 0, 512, "x01")
+        nc.sync.dma_start(out=w0_codes[:].bitcast(I32), in_=w0_words[0].bitcast(I32))
+        nc.sync.dma_start(out=w1_codes[:].bitcast(I32), in_=w1_words[0].rearrange("p n i -> p (n i)").bitcast(I32))
+        load_scales(nc.sync, w1_scale, w1_scales)
+        x2 = load(x_rows, 512, 768, "x2")
+        w2a = load(w2_rows, 0, 256, "w2a")
+        x3 = load(x_rows, 768, 1024, "x3")
+        w2b = load(w2_rows, 256, 512, "w2b")
+        x4 = load(x_rows, 1024, 1280, "x4")
+        x5 = load(x_rows, 1280, 1536, "x5")
+
+        bias_ps = ps.tile([P, P], F32, tag="bank7")
+        nc.tensor.transpose(bias_ps[:], bias_rows[:], ident[:])
+        nc.scalar.copy(out=bias[:], in_=bias_ps[:, 0:M_TILES])
+
+        prepare(x01, x_codes, x_scale, 0, "p01")
+        g0 = [ps.tile([P, 512], F32, name="g0_%d" % m, tag="bank%d" % m) for m in range(M_TILES)]
+        for m in range(M_TILES):
+            tap(g0[m], 0, 0, m, 0, 512, start=True)
+        for m in range(M_TILES):
+            tap(g0[m], 0, 1, m, 0, 256)
+
+        prepare(x2, x_codes, x_scale, 512, "p2")
+        g1 = [ps.tile([P, 256], F32, name="g1_%d" % m, tag="bank%d" % (4 + m)) for m in range(M_TILES)]
+        for m in range(M_TILES):
+            tap(g0[m], 0, 1, m, 256, 512)
+        for m in range(M_TILES):
+            tap(g1[m], 512, 0, m, 512, 640, start=True)
+            tap(g1[m], 512, 0, m, 640, 768)
+
+        prepare(w2a, w2_codes, w2_scale, 0, "pw2a")
+        for m in range(2):
+            tap(g0[m], 0, 2, m, 0, 256)
+
+        prepare(x3, x_codes, x_scale, 768, "p3")
+        for m in range(2):
+            tap(g0[m], 0, 2, m, 256, 512, stop=True)
+        for m in range(M_TILES):
+            tap(g1[m], 512, 1, m, 512, 768)
+        finish(g0, 0, 2, 0, 512, "r0a")
+
+        prepare(w2b, w2_codes, w2_scale, 256, "pw2b")
+        for m in range(2, M_TILES):
+            tap(g0[m], 0, 2, m, 0, 512, stop=True)
+        finish(g0, 2, 4, 0, 512, "r0b")
+
+        g2 = [ps.tile([P, 256], F32, name="g2_%d" % m, tag="bank%d" % m) for m in range(M_TILES)]
+        for m in range(2):
+            tap(g2[m], 768, 0, m, 768, 896, start=True)
+            tap(g2[m], 768, 0, m, 896, 1024)
+
+        prepare(x4, x_codes, x_scale, 1024, "p4")
+        for m in range(M_TILES):
+            tap(g1[m], 512, 2, m, 512, 768, stop=True)
+        finish(g1, 0, 4, 512, 768, "r1")
+        for m in range(2):
+            tap(g2[m], 768, 1, m, 768, 1024)
+        for m in range(2, M_TILES):
+            tap(g2[m], 768, 0, m, 768, 896, start=True)
+            tap(g2[m], 768, 0, m, 896, 1024)
+            tap(g2[m], 768, 1, m, 768, 1024)
+
+        prepare(x5, x_codes, x_scale, 1280, "p5")
+        for m in range(M_TILES):
+            tap(g2[m], 768, 2, m, 768, 1024, stop=True)
+        finish(g2, 0, 2, 768, 1024, "r2a")
+        finish(g2, 2, 4, 768, 1024, "r2b")

@@ -1,7 +1,6 @@
 from contextlib import ExitStack
 
 import concourse.mybir as mybir
-from concourse.masks import make_identity
 
 D, K, M, T = 256, 512, 512, 1024
 FLOPS = 2 * 3 * K * M * T
@@ -40,9 +39,8 @@ def tile_mix_dconv_fm_silu_kernel(tc, x, w0_words, w0_scales, w1_words, w1_scale
         w1_scale = sb.tile([P, M], U8, align_bytes=64)
         w2_codes = sb.tile([P, M], U32, align_bytes=64)
         w2_scale = sb.tile([P, M], U8, align_bytes=64)
-        bias_rows = sb.tile([P, P], F32)
-        bias = sb.tile([P, M_TILES], F32)
-        ident = sb.tile([P, P], F32)
+        bias_rows = sb.tile([P, P], F32, align_bytes=64)
+        bias = sb.tile([P, P], F32, align_bytes=64)
         warm = sb.tile([P, 1], F32)
 
         def load(rows, c0, c1, name):
@@ -50,27 +48,22 @@ def tile_mix_dconv_fm_silu_kernel(tc, x, w0_words, w0_scales, w1_words, w1_scale
             nc.sync.dma_start(out=raw[:], in_=rows[:, :, c0:c1])
             return raw
 
-        def load_scales(queue, plane, scales):
+        def load_scales(plane, scales):
             for r in range(4):
-                queue.dma_start(out=plane[r:P:32, :].bitcast(I32), in_=scales[0, r:16:4, :].bitcast(I32))
+                nc.sync.dma_start(out=plane[r:P:32, :].bitcast(I32), in_=scales[0, r:16:4, :].bitcast(I32))
 
-        def interleave(raw, c0, c1, name):
-            packed = sb.tile([P, PACK * (c1 - c0)], BF16, name=name, align_bytes=64)
-            nc.vector.tensor_copy(
-                out=packed[:].rearrange("p (c i j) -> p c j i", i=4, j=PACK),
-                in_=raw[:, :, c0:c1].rearrange("p j (c i) -> p c j i", i=4),
+        def interleave(copy, packed, raw, r0, p0, width):
+            copy(
+                out=packed[:, PACK * p0:PACK * (p0 + width)].rearrange("p (c i j) -> p c j i", i=4, j=PACK),
+                in_=raw[:, :, r0:r0 + width].rearrange("p j (c i) -> p c j i", i=4),
             )
-            return packed
+
+        def packed_tile(width, name):
+            return sb.tile([P, PACK * width], BF16, name=name, align_bytes=64)
 
         def quantise(packed, codes, scale, c0):
             cols = slice(c0, c0 + packed.shape[1] // PACK)
             nc.vector.quantize_mx(out=codes[:, cols].bitcast(FP8X4), scales=scale[:, cols], in_=packed[:])
-
-        def prepare(raw, codes, scale, c0, name):
-            half = raw.shape[2] // 2
-            packed = [interleave(raw, h * half, (h + 1) * half, "%s_%d" % (name, h)) for h in range(2)]
-            for h in range(2):
-                quantise(packed[h], codes, scale, c0 + h * half)
 
         def tap(acc, t_base, which, m, t0, t1, start=False, stop=False):
             m_cols = slice(m * P, (m + 1) * P)
@@ -89,82 +82,76 @@ def tile_mix_dconv_fm_silu_kernel(tc, x, w0_words, w0_scales, w1_words, w1_scale
         def finish(accs, m0, m1, t0, t1, name):
             res = sb.tile([P, m1 - m0, t1 - t0], F32, name=name)
             for m in range(m0, m1):
-                nc.scalar.activation(out=res[:, m - m0, :], in_=accs[m][:], func=SILU, bias=bias[:, m:m + 1])
+                nc.scalar.activation(out=res[:, m - m0, :], in_=accs[m][:], func=SILU, bias=bias[:, 32 * m:32 * m + 1])
             nc.sync.dma_start(out=out_tiles[:, m0:m1, t0:t1], in_=res[:])
 
-        nc.vector.memset(bias_rows[:], 0.0)
+        def prepare_wide(raw, c0, name):
+            first, second = packed_tile(256, name + "_0"), packed_tile(256, name + "_1")
+            interleave(nc.scalar.copy, second, raw, 256 + 64, 64, 192)
+            interleave(nc.vector.tensor_copy, first, raw, 0, 0, 256)
+            interleave(nc.vector.tensor_copy, second, raw, 256, 0, 64)
+            quantise(first, x_codes, x_scale, c0)
+            quantise(second, x_codes, x_scale, c0 + 256)
+
+        def prepare_narrow(raw, c0, name):
+            packed = [packed_tile(128, "%s_%d" % (name, h)) for h in range(2)]
+            for h in range(2):
+                interleave(nc.vector.tensor_copy, packed[h], raw, 128 * h, 0, 128)
+            for h in range(2):
+                quantise(packed[h], x_codes, x_scale, c0 + 128 * h)
+
         nc.vector.memset(w0_scale[:].bitcast(I32), 0)
+        nc.vector.memset(bias_rows[:], 0.0)
         nc.vector.memset(w1_scale[:].bitcast(I32), 0)
         nc.vector.memset(warm[:], 0.0)
         nc.scalar.activation(out=warm[:], in_=warm[:], func=SILU)
-        make_identity(nc, ident[:])
-        nc.gpsimd.dma_start(out=bias_rows[0:M_TILES, :], in_=b.rearrange("(m p) -> m p", p=P))
-        load_scales(nc.gpsimd, w0_scale, w0_scales)
 
-        x01 = load(x_rows, 0, 512, "x01")
+        xa = load(x_rows, 0, 512, "xa")
         nc.sync.dma_start(out=w0_codes[:].bitcast(I32), in_=w0_words[0].bitcast(I32))
+        load_scales(w0_scale, w0_scales)
+        nc.sync.dma_start(
+            out=bias_rows[0:P:32, :].rearrange("q (m i) -> q m i", i=32),
+            in_=b.rearrange("(m q i) -> q m i", q=4, i=32),
+        )
+        xb = load(x_rows, 512, 1024, "xb")
         nc.sync.dma_start(out=w1_codes[:].bitcast(I32), in_=w1_words[0].rearrange("p n i -> p (n i)").bitcast(I32))
-        load_scales(nc.sync, w1_scale, w1_scales)
-        x2 = load(x_rows, 512, 768, "x2")
-        w2a = load(w2_rows, 0, 256, "w2a")
-        x3 = load(x_rows, 768, 1024, "x3")
-        w2b = load(w2_rows, 256, 512, "w2b")
+        load_scales(w1_scale, w1_scales)
+        w2_raw = load(w2_rows, 0, M, "w2_raw")
         x4 = load(x_rows, 1024, 1280, "x4")
         x5 = load(x_rows, 1280, 1536, "x5")
 
-        bias_ps = ps.tile([P, P], F32, tag="bank7")
-        nc.tensor.transpose(bias_ps[:], bias_rows[:], ident[:])
-        nc.scalar.copy(out=bias[:], in_=bias_ps[:, 0:M_TILES])
+        g0 = [ps.tile([P, 512], F32, name="g0_%d" % m) for m in range(M_TILES)]
+        g1 = [ps.tile([P, 512], F32, name="g1_%d" % m) for m in range(M_TILES)]
 
-        prepare(x01, x_codes, x_scale, 0, "p01")
-        g0 = [ps.tile([P, 512], F32, name="g0_%d" % m, tag="bank%d" % m) for m in range(M_TILES)]
+        prepare_wide(xa, 0, "pa")
+        nc.vector.transpose(bias[:], bias_rows[:])
         for m in range(M_TILES):
             tap(g0[m], 0, 0, m, 0, 512, start=True)
-        for m in range(M_TILES):
-            tap(g0[m], 0, 1, m, 0, 256)
 
-        prepare(x2, x_codes, x_scale, 512, "p2")
-        g1 = [ps.tile([P, 256], F32, name="g1_%d" % m, tag="bank%d" % (4 + m)) for m in range(M_TILES)]
+        prepare_wide(xb, 512, "pb")
         for m in range(M_TILES):
-            tap(g0[m], 0, 1, m, 256, 512)
+            tap(g0[m], 0, 1, m, 0, 512)
         for m in range(M_TILES):
-            tap(g1[m], 512, 0, m, 512, 640, start=True)
-            tap(g1[m], 512, 0, m, 640, 768)
+            tap(g1[m], 512, 0, m, 512, 1024, start=True)
 
-        prepare(w2a, w2_codes, w2_scale, 0, "pw2a")
-        for m in range(2):
-            tap(g0[m], 0, 2, m, 0, 256)
+        w2_packed = [packed_tile(P, "pw2_%d" % m) for m in range(M_TILES)]
+        for m in range(M_TILES):
+            interleave(nc.vector.tensor_copy if m < 2 else nc.scalar.copy, w2_packed[m], w2_raw, P * m, 0, P)
+        for m in range(M_TILES):
+            quantise(w2_packed[m], w2_codes, w2_scale, P * m)
+        for m in range(M_TILES):
+            tap(g0[m], 0, 2, m, 0, 512, stop=True)
+            finish(g0, m, m + 1, 0, 512, "r0_%d" % m)
 
-        prepare(x3, x_codes, x_scale, 768, "p3")
-        for m in range(2):
-            tap(g0[m], 0, 2, m, 256, 512, stop=True)
         for m in range(M_TILES):
             tap(g1[m], 512, 1, m, 512, 768)
-        finish(g0, 0, 2, 0, 512, "r0a")
 
-        prepare(w2b, w2_codes, w2_scale, 256, "pw2b")
-        for m in range(2, M_TILES):
-            tap(g0[m], 0, 2, m, 0, 512, stop=True)
-        finish(g0, 2, 4, 0, 512, "r0b")
-
-        g2 = [ps.tile([P, 256], F32, name="g2_%d" % m, tag="bank%d" % m) for m in range(M_TILES)]
-        for m in range(2):
-            tap(g2[m], 768, 0, m, 768, 896, start=True)
-            tap(g2[m], 768, 0, m, 896, 1024)
-
-        prepare(x4, x_codes, x_scale, 1024, "p4")
+        prepare_narrow(x4, 1024, "p4")
         for m in range(M_TILES):
-            tap(g1[m], 512, 2, m, 512, 768, stop=True)
-        finish(g1, 0, 4, 512, 768, "r1")
-        for m in range(2):
-            tap(g2[m], 768, 1, m, 768, 1024)
-        for m in range(2, M_TILES):
-            tap(g2[m], 768, 0, m, 768, 896, start=True)
-            tap(g2[m], 768, 0, m, 896, 1024)
-            tap(g2[m], 768, 1, m, 768, 1024)
+            tap(g1[m], 512, 1, m, 768, 1024)
+            tap(g1[m], 512, 2, m, 512, 768)
 
-        prepare(x5, x_codes, x_scale, 1280, "p5")
+        prepare_narrow(x5, 1280, "p5")
         for m in range(M_TILES):
-            tap(g2[m], 768, 2, m, 768, 1024, stop=True)
-        finish(g2, 0, 2, 768, 1024, "r2a")
-        finish(g2, 2, 4, 768, 1024, "r2b")
+            tap(g1[m], 512, 2, m, 768, 1024, stop=True)
+            finish(g1, m, m + 1, 512, 1024, "r1_%d" % m)

@@ -114,14 +114,14 @@ def tile_mix_dconv_fm_silu_kernel(tc, x, w0_words, w0_scales, w1_words, w1_scale
             in_=b.rearrange("(m q i) -> q m i", q=4, i=32),
         )
         xb = load(x_rows, 512, 1024, "xb")
-        nc.sync.dma_start(out=w1_codes[:].bitcast(I32), in_=w1_words[0].rearrange("p n i -> p (n i)").bitcast(I32))
-        load_scales(w1_scale, w1_scales)
         w2_raw = load(w2_rows, 0, M, "w2_raw")
+        load_scales(w1_scale, w1_scales)
+        nc.sync.dma_start(out=w1_codes[:].bitcast(I32), in_=w1_words[0].rearrange("p n i -> p (n i)").bitcast(I32))
         x4 = load(x_rows, 1024, 1280, "x4")
         x5 = load(x_rows, 1280, 1536, "x5")
 
-        g0 = [ps.tile([P, 512], F32, name="g0_%d" % m) for m in range(M_TILES)]
-        g1 = [ps.tile([P, 512], F32, name="g1_%d" % m) for m in range(M_TILES)]
+        g0 = [ps.tile([P, 512], F32, name="g0_%d" % m, tag="bank%d" % m) for m in range(M_TILES)]
+        g1 = [ps.tile([P, 256 if m < 2 else 512], F32, name="g1_%d" % m, tag="bank%d" % (4 + m)) for m in range(M_TILES)]
 
         prepare_wide(xa, 0, "pa")
         nc.vector.transpose(bias[:], bias_rows[:])
@@ -129,29 +129,43 @@ def tile_mix_dconv_fm_silu_kernel(tc, x, w0_words, w0_scales, w1_words, w1_scale
             tap(g0[m], 0, 0, m, 0, 512, start=True)
 
         prepare_wide(xb, 512, "pb")
-        for m in range(M_TILES):
-            tap(g0[m], 0, 1, m, 0, 512)
-        for m in range(M_TILES):
+        for m in range(2):
+            tap(g1[m], 512, 0, m, 512, 640, start=True)
+            tap(g1[m], 512, 0, m, 640, 768)
+        for m in range(2, M_TILES):
             tap(g1[m], 512, 0, m, 512, 1024, start=True)
 
         w2_packed = [packed_tile(P, "pw2_%d" % m) for m in range(M_TILES)]
+        interleave(nc.scalar.copy, w2_packed[3], w2_raw, P * 3, 0, P)
+        interleave(nc.vector.tensor_copy, w2_packed[0], w2_raw, 0, 0, P)
         for m in range(M_TILES):
-            interleave(nc.vector.tensor_copy if m < 2 else nc.scalar.copy, w2_packed[m], w2_raw, P * m, 0, P)
-        for m in range(M_TILES):
+            if m < 2:
+                interleave(nc.vector.tensor_copy, w2_packed[m + 1], w2_raw, P * (m + 1), 0, P)
             quantise(w2_packed[m], w2_codes, w2_scale, P * m)
         for m in range(M_TILES):
+            tap(g0[m], 0, 1, m, 0, 512)
             tap(g0[m], 0, 2, m, 0, 512, stop=True)
             finish(g0, m, m + 1, 0, 512, "r0_%d" % m)
 
-        for m in range(M_TILES):
-            tap(g1[m], 512, 1, m, 512, 768)
-
         prepare_narrow(x4, 1024, "p4")
-        for m in range(M_TILES):
-            tap(g1[m], 512, 1, m, 768, 1024)
-            tap(g1[m], 512, 2, m, 512, 768)
+        for m in range(2):
+            tap(g1[m], 512, 1, m, 512, 768)
+            tap(g1[m], 512, 2, m, 512, 768, stop=True)
+        finish(g1, 0, 2, 512, 768, "r1_early")
+        g2 = [ps.tile([P, 256], F32, name="g2_%d" % m, tag="bank%d" % m) for m in range(2)]
+        for m in range(2):
+            tap(g2[m], 768, 0, m, 768, 896, start=True)
+            tap(g2[m], 768, 0, m, 896, 1024)
+            tap(g2[m], 768, 1, m, 768, 1024)
+        tap(g1[2], 512, 1, 2, 512, 1024)
+        tap(g1[2], 512, 2, 2, 512, 768)
 
         prepare_narrow(x5, 1280, "p5")
-        for m in range(M_TILES):
-            tap(g1[m], 512, 2, m, 768, 1024, stop=True)
-            finish(g1, m, m + 1, 512, 1024, "r1_%d" % m)
+        for m in range(2):
+            tap(g2[m], 768, 2, m, 768, 1024, stop=True)
+            finish(g2, m, m + 1, 768, 1024, "r2_%d" % m)
+        tap(g1[2], 512, 2, 2, 768, 1024, stop=True)
+        finish(g1, 2, 3, 512, 1024, "r1_2")
+        tap(g1[3], 512, 1, 3, 512, 1024)
+        tap(g1[3], 512, 2, 3, 512, 1024, stop=True)
+        finish(g1, 3, 4, 512, 1024, "r1_3")

from contextlib import ExitStack

import concourse.mybir as mybir

D, K, M, T = 256, 512, 512, 1024
FLOPS = 2 * 3 * K * M * T

F32 = mybir.dt.float32
BF16 = mybir.dt.bfloat16
I32 = mybir.dt.int32
U32 = mybir.dt.uint32
U8 = mybir.dt.uint8
FP8X4 = mybir.dt.float8_e4m3fn_x4
FP4X4 = mybir.dt.float4_e2m1fn_x4
SILU = mybir.ActivationFunctionType.Silu

P = 128
PACK = 4
M_TILES = M // P
X_COLS = T + 2 * D


def tile_mix_dconv_fm_silu_kernel(tc, x, w0_words, w0_scales, w1_words, w1_scales, w2, b, out):
    nc = tc.nc
    x_rows = x.rearrange("(p j) t -> p j t", j=PACK)
    w2_rows = w2.rearrange("(p j) n -> p j n", j=PACK)
    out_tiles = out.rearrange("(m p) t -> p m t", p=P)

    with ExitStack() as ctx:
        sb = ctx.enter_context(tc.tile_pool(name="sb", bufs=1))
        ps = ctx.enter_context(tc.psum_pool(name="ps", bufs=1))
        ctx.enter_context(tc.manual_schedule())

        x_codes = sb.tile([P, X_COLS], U32, align_bytes=64)
        x_scale = sb.tile([P, X_COLS], U8, align_bytes=64)
        w0_codes = sb.tile([P, 2 * M], U8, align_bytes=64)
        w0_scale = sb.tile([P, M], U8, align_bytes=64)
        w1_codes = sb.tile([P, M], U32, align_bytes=64)
        w1_scale = sb.tile([P, M], U8, align_bytes=64)
        w2_codes = sb.tile([P, M], U32, align_bytes=64)
        w2_scale = sb.tile([P, M], U8, align_bytes=64)
        bias_rows = sb.tile([P, P], F32, align_bytes=64)
        bias = sb.tile([P, P], F32, align_bytes=64)
        warm = sb.tile([P, 1], F32)

        def load(rows, c0, c1, name):
            raw = sb.tile([P, PACK, c1 - c0], F32, name=name)
            nc.sync.dma_start(out=raw[:], in_=rows[:, :, c0:c1])
            return raw

        def load_scales(plane, scales):
            for r in range(4):
                nc.sync.dma_start(out=plane[r:P:32, :].bitcast(I32), in_=scales[0, r:16:4, :].bitcast(I32))

        def interleave(copy, packed, raw, r0, p0, width):
            copy(
                out=packed[:, PACK * p0:PACK * (p0 + width)].rearrange("p (c i j) -> p c j i", i=4, j=PACK),
                in_=raw[:, :, r0:r0 + width].rearrange("p j (c i) -> p c j i", i=4),
            )

        def packed_tile(width, name):
            return sb.tile([P, PACK * width], BF16, name=name, align_bytes=64)

        def quantise(packed, codes, scale, c0):
            cols = slice(c0, c0 + packed.shape[1] // PACK)
            nc.vector.quantize_mx(out=codes[:, cols].bitcast(FP8X4), scales=scale[:, cols], in_=packed[:])

        def tap(acc, t_base, which, m, t0, t1, start=False, stop=False):
            m_cols = slice(m * P, (m + 1) * P)
            if which == 0:
                lhs, lhs_scale = w0_codes[:, 2 * m * P:2 * (m + 1) * P].bitcast(FP4X4), w0_scale[:, m_cols]
            elif which == 1:
                lhs, lhs_scale = w1_codes[:, m_cols].bitcast(FP8X4), w1_scale[:, m_cols]
            else:
                lhs, lhs_scale = w2_codes[:, m_cols].bitcast(FP8X4), w2_scale[:, m_cols]
            x_cols = slice(t0 + which * D, t1 + which * D)
            nc.tensor.matmul_mx(
                out=acc[:, t0 - t_base:t1 - t_base], lhsT=lhs, lhsT_scale=lhs_scale,
                rhs=x_codes[:, x_cols].bitcast(FP8X4), rhs_scale=x_scale[:, x_cols], start=start, stop=stop,
            )

        def finish(accs, m0, m1, t0, t1, name):
            res = sb.tile([P, m1 - m0, t1 - t0], F32, name=name)
            for m in range(m0, m1):
                nc.scalar.activation(out=res[:, m - m0, :], in_=accs[m][:], func=SILU, bias=bias[:, 32 * m:32 * m + 1])
            nc.sync.dma_start(out=out_tiles[:, m0:m1, t0:t1], in_=res[:])

        def prepare_wide(raw, c0, name):
            first, second = packed_tile(256, name + "_0"), packed_tile(256, name + "_1")
            interleave(nc.scalar.copy, second, raw, 256 + 64, 64, 192)
            interleave(nc.vector.tensor_copy, first, raw, 0, 0, 256)
            interleave(nc.vector.tensor_copy, second, raw, 256, 0, 64)
            quantise(first, x_codes, x_scale, c0)
            quantise(second, x_codes, x_scale, c0 + 256)

        def prepare_narrow(raw, c0, name):
            packed = [packed_tile(128, "%s_%d" % (name, h)) for h in range(2)]
            for h in range(2):
                interleave(nc.vector.tensor_copy, packed[h], raw, 128 * h, 0, 128)
            for h in range(2):
                quantise(packed[h], x_codes, x_scale, c0 + 128 * h)

        nc.vector.memset(w0_scale[:].bitcast(I32), 0)
        nc.vector.memset(bias_rows[:], 0.0)
        nc.vector.memset(w1_scale[:].bitcast(I32), 0)
        nc.vector.memset(warm[:], 0.0)
        nc.scalar.activation(out=warm[:], in_=warm[:], func=SILU)

        xa = load(x_rows, 0, 512, "xa")
        nc.sync.dma_start(out=w0_codes[:].bitcast(I32), in_=w0_words[0].bitcast(I32))
        load_scales(w0_scale, w0_scales)
        nc.sync.dma_start(
            out=bias_rows[0:P:32, :].rearrange("q (m i) -> q m i", i=32),
            in_=b.rearrange("(m q i) -> q m i", q=4, i=32),
        )
        xb = load(x_rows, 512, 1024, "xb")
        w2_raw = load(w2_rows, 0, M, "w2_raw")
        load_scales(w1_scale, w1_scales)
        nc.sync.dma_start(out=w1_codes[:].bitcast(I32), in_=w1_words[0].rearrange("p n i -> p (n i)").bitcast(I32))
        x4 = load(x_rows, 1024, 1280, "x4")
        x5 = load(x_rows, 1280, 1536, "x5")

        g0 = [ps.tile([P, 512], F32, name="g0_%d" % m, tag="bank%d" % m) for m in range(M_TILES)]
        g1 = [ps.tile([P, 256 if m < 2 else 512], F32, name="g1_%d" % m, tag="bank%d" % (4 + m)) for m in range(M_TILES)]

        prepare_wide(xa, 0, "pa")
        nc.vector.transpose(bias[:], bias_rows[:])
        for m in range(M_TILES):
            tap(g0[m], 0, 0, m, 0, 512, start=True)

        prepare_wide(xb, 512, "pb")
        for m in range(2):
            tap(g1[m], 512, 0, m, 512, 640, start=True)
            tap(g1[m], 512, 0, m, 640, 768)
        for m in range(2, M_TILES):
            tap(g1[m], 512, 0, m, 512, 1024, start=True)

        w2_packed = [packed_tile(P, "pw2_%d" % m) for m in range(M_TILES)]
        interleave(nc.scalar.copy, w2_packed[3], w2_raw, P * 3, 0, P)
        interleave(nc.vector.tensor_copy, w2_packed[0], w2_raw, 0, 0, P)
        for m in range(M_TILES):
            if m < 2:
                interleave(nc.vector.tensor_copy, w2_packed[m + 1], w2_raw, P * (m + 1), 0, P)
            quantise(w2_packed[m], w2_codes, w2_scale, P * m)
        for m in range(M_TILES):
            tap(g0[m], 0, 1, m, 0, 512)
            tap(g0[m], 0, 2, m, 0, 512, stop=True)
            finish(g0, m, m + 1, 0, 512, "r0_%d" % m)

        prepare_narrow(x4, 1024, "p4")
        for m in range(2):
            tap(g1[m], 512, 1, m, 512, 768)
            tap(g1[m], 512, 2, m, 512, 768, stop=True)
        finish(g1, 0, 2, 512, 768, "r1_early")
        g2 = [ps.tile([P, 256], F32, name="g2_%d" % m, tag="bank%d" % m) for m in range(2)]
        for m in range(2):
            tap(g2[m], 768, 0, m, 768, 896, start=True)
            tap(g2[m], 768, 0, m, 896, 1024)
            tap(g2[m], 768, 1, m, 768, 1024)
        tap(g1[2], 512, 1, 2, 512, 1024)
        tap(g1[2], 512, 2, 2, 512, 768)

        prepare_narrow(x5, 1280, "p5")
        for m in range(2):
            tap(g2[m], 768, 2, m, 768, 1024, stop=True)
            finish(g2, m, m + 1, 768, 1024, "r2_%d" % m)
        tap(g1[2], 512, 2, 2, 768, 1024, stop=True)
        finish(g1, 2, 3, 512, 1024, "r1_2")
        tap(g1[3], 512, 1, 3, 512, 1024)
        tap(g1[3], 512, 2, 3, 512, 1024, stop=True)
        finish(g1, 3, 4, 512, 1024, "r1_3")
